import numpy as np, ml_dtypes
CORES = [0,1,2,3,4,5,6,7]
N = 8
ROOT = 7
def setup_inputs(rng):
    return {"x": rng.standard_normal((N, 128, 1024), dtype=np.float32).astype(ml_dtypes.bfloat16)}
def reference(x):
    y = np.full(x.shape, np.nan, x.dtype)
    y[ROOT] = x.sum(axis=0, dtype=np.float64).astype(x.dtype)
    return {"y": y}

from concourse.bass import DstId, RemoteDMATransfer
from concourse.mybir import AluOpType

ROOT = 7
OWNERS = 7
NA, RA = 2, 19
NB, RB = 5, 18
SPLIT = NA * RA

SCRATCH = {
    "xa": ("dram", [NA, 128, 8 * RA], "bfloat16"),
    "xb": ("dram", [NB, 128, 8 * RB], "bfloat16"),
    "la": ("dram", [OWNERS - 1, 128, 8 * RA], "bfloat16"),
    "lb": ("dram", [OWNERS - 1, 128, 8 * RB], "bfloat16"),
    "ra": ("dram", [NA, 128, 8 * RA], "bfloat16"),
    "rb": ("dram", [NB, 128, 8 * RB], "bfloat16"),
}
SEMAPHORES = ["loaded_a", "loaded_b", "sent", "arrived", "done", "stored"]


def exchange_plan(c):
    wide = [p for p in range(NA) if p != c]
    narrow = [p for p in [NA + (c + k) % NB for k in range(NB)] if p != c]
    if len(wide) == 2:
        wide_calls = [[(wide[0], 0x00FF), (wide[1], 0xFF00)]]
    else:
        wide_calls = [[(wide[0], 0xFFFF)]]
    narrow_calls = [[(p, 0xF << (4 * j)) for j, p in enumerate(narrow[:4])]]
    if len(narrow) == 5:
        narrow_calls.append([(narrow[4], 0xFFFF)])
    return wide_calls, narrow_calls


def engines(mask):
    return bin(mask).count("1")


def rank_program(g, core, T, topo):
    if T.rank_of(core) is None:
        return

    if core == ROOT:
        g.sync.dma_start(T.y[:, :], T.x[:, :]).then_inc(T.sem.loaded_a, 16)
        g.wait_ge(T.sem.loaded_a, 16)
        g.wait_ge(T.sem.done, OWNERS * 16)
        g.dma_start(T.y[0:SPLIT, :], T.ra[:, :, :], accum_op=AluOpType.add,
                    max_dma_last_dim=4096).then_inc(T.sem.stored, 16)
        g.dma_start(T.y[SPLIT:128, :], T.rb[:, :, :], accum_op=AluOpType.add,
                    max_dma_last_dim=4096).then_inc(T.sem.stored, 16)
        g.wait_ge(T.sem.stored, 32)
        return

    def dst_id(c):
        rid, pid, _sengine = topo.addr(c)
        return DstId(rid=rid, pnc=pid)

    def piece(a, b, p):
        return a[p] if p < NA else b[p - NA]

    def send(calls):
        for call in calls:
            transfers = []
            for p, mask in call:
                slot = core if core < p else core - 1
                transfers.append(RemoteDMATransfer(
                    dst_ids=[dst_id(p)], dma_engine_mask=mask & topo.mask(core, p), remote_sem=T.sem.arrived,
                    src=piece(T.xa, T.xb, p), dst=(T.la if p < NA else T.lb)[slot]))
            g.remote_dma_fused(transfers, local_sem=T.sem.sent)

    g.sync.dma_start(T.xa[:, :, :], T.x[0:SPLIT, :]).then_inc(T.sem.loaded_a, 16)
    g.scalar.dma_start(T.xb[:, :, :], T.x[SPLIT:128, :]).then_inc(T.sem.loaded_b, 16)

    wide_calls, narrow_calls = exchange_plan(core)
    g.wait_ge(T.sem.loaded_a, 16)
    send(wide_calls)
    g.wait_ge(T.sem.loaded_b, 16)
    send(narrow_calls)

    expected = 0
    for c in range(OWNERS):
        if c != core:
            wc, nc = exchange_plan(c)
            expected += sum(engines(m) for call in wc + nc for p, m in call if p == core)
    g.wait_ge(T.sem.arrived, expected)
    land = T.la if core < NA else T.lb
    g.remote_dma_fused([RemoteDMATransfer(
        dst_ids=[dst_id(ROOT)], dma_engine_mask=topo.mask(core, ROOT), remote_sem=T.sem.done,
        srcs=[piece(T.xa, T.xb, core)] + [land[s] for s in range(OWNERS - 1)],
        dsts=[piece(T.ra, T.rb, core)], alu_op=1)], local_sem=T.sem.sent)

    g.wait_ge(T.sem.sent, 16 * (len(wide_calls) + len(narrow_calls) + 1))
